import numpy as np, ml_dtypes
CORES = [5,29,101,125,133,157,229,253]
N = 8
import mx_ref
NC, G, D = 384, 4, 64
C = np.float32(0.037)
BF = ml_dtypes.bfloat16
def cut(t, i, w=512):
    return t[:, w * i:w * i + w]
def tile(rs):
    return np.stack(rs, axis=2).reshape(128, -1).astype(BF)
def layer(w, X):
    out = []
    for i in range(G):
        for t in range(len(X)):
            p = mx_ref.matmul(mx_ref.quantize(cut(w, len(X) * i + t)), X[t])
            z = p if t == 0 else z + p
        out.append(z)
    return out
def act(Z):
    return [np.maximum(z, 0) * C for z in Z]
def setup_inputs(rng):
    def f(*shape):
        return mx_ref.flush((rng.standard_normal(shape, dtype=np.float32) * np.exp2(rng.integers(-2, 3, shape[:-1] + (1,)))).astype(BF))
    return {"x": f(N, 128, 4 * NC), "w1": np.broadcast_to(f(1, 128, G * 512), (N, 128, G * 512)).copy(), "wt": f(N, 128, 3 * 512)}
def setup_inputs_blocks(rng):
    d = setup_inputs(rng)
    for k in ("x", "wt"): d[k] = mx_ref.spread(d[k], rng, 2)
    return d
def setup_inputs_wide(rng):
    d = setup_inputs(rng)
    for k in ("wt",): d[k] = mx_ref.flush((d[k].astype(np.float32) * np.exp2(rng.integers(-6, 7, (N, 1, 1))).astype(np.float32)).astype(BF))
    return d
def setup_inputs_zeros(rng):
    d = setup_inputs(rng); v = d["x"].reshape(N, 128, -1, 4).copy()
    v[np.broadcast_to((rng.random((N, 1, v.shape[2], 1)) < 0.33), v.shape)] = 0
    d["x"] = v.reshape(d["x"].shape)
    return d
def reference(x, w1, wt):
    h = [tile(act(layer(w1[j], [mx_ref.quantize(x[j])]))) for j in range(N)]
    y = np.zeros((N, 128, NC), np.float32)
    for r in range(N):
        e = np.concatenate([h[(r - 1) % N][:, 4 * (NC - D):], h[r], h[(r + 1) % N][:, :4 * D]], axis=1)
        for t in range(3):
            p = mx_ref.matmul(mx_ref.quantize(cut(wt[r], t)), mx_ref.quantize(e[:, 4 * D * t:4 * D * t + 4 * NC]))
            y[r] = p if t == 0 else y[r] + p
    return {"y": y}

import numpy as np
from concourse.bass import DstId, RemoteDMATransfer
from concourse.mybir import dt, AluOpType, ActivationFunctionType

NC, D = 384, 64
H = 2 * D
C = float(np.float32(0.037))

SCRATCH = {
    "xh": ("sbuf", [128, 4 * H], "bfloat16"),
    "xo": ("sbuf", [128, 4 * NC], "bfloat16"),
    "w1s": ("sbuf", [128, 2048], "bfloat16"),
    "wts": ("sbuf", [128, 1536], "bfloat16"),
    "h": ("sbuf", [128, 4 * NC], "bfloat16"),
    "hh": ("sbuf", [128, 4 * H], "bfloat16"),
    "qxh": ("sbuf", [128, H], "float8_e4m3fn_x4"), "sxh": ("sbuf", [128, H], "uint8"),
    "qx": ("sbuf", [128, NC], "float8_e4m3fn_x4"), "sx": ("sbuf", [128, NC], "uint8"),
    "qw": ("sbuf", [128, 512], "float8_e4m3fn_x4"), "sw": ("sbuf", [128, 512], "uint8"),
    "qt": ("sbuf", [128, NC], "float8_e4m3fn_x4"), "st": ("sbuf", [128, NC], "uint8"),
    "qh": ("sbuf", [128, NC], "float8_e4m3fn_x4"), "sh": ("sbuf", [128, NC], "uint8"),
    "qr": ("sbuf", [128, H], "float8_e4m3fn_x4"), "sr": ("sbuf", [128, H], "uint8"),
    "qhh": ("sbuf", [128, H], "float8_e4m3fn_x4"), "shh": ("sbuf", [128, H], "uint8"),
    "rc": ("sbuf", [128, D], "float8_e4m3fn_x4"), "rp": ("sbuf", [128, D], "uint8"),
    "ya": ("sbuf", [128, NC - H], "float32"), "yb": ("sbuf", [128, D], "float32"), "yc": ("sbuf", [128, D], "float32"),
    "zp": ("psum", [128, 2048], "float32"), "zh": ("psum", [128, 2048], "float32"),
}
SEMAPHORES = (["lxh", "lw0", "lw1", "lx", "lwt", "qxh", "qx", "qh", "qwt", "qhh", "act", "acth", "iss", "loc", "rel", "arr",
               "mA", "mB", "mC", "cA", "cB", "cC", "oAB", "oC"]
              + ["qw%d" % i for i in range(4)] + ["z%d" % i for i in range(4)] + ["zh%d" % i for i in range(4)])


def engines(mask, first, count):
    bits = [b for b in range(16) if mask >> b & 1][first:first + count]
    return sum(1 << b for b in bits)


def plan(r, T, topo):
    n = len(T.cores)
    me, left, right = T.cores[r], (r - 1) % n, (r + 1) % n
    first = me
    while first and (topo.host(first - 1), topo.chip(first - 1)) == (topo.host(me), topo.chip(me)):
        first -= 1
    chip = [first]
    while (topo.host(chip[-1] + 1), topo.chip(chip[-1] + 1)) == (topo.host(me), topo.chip(me)):
        chip.append(chip[-1] + 1)
    able = [c for c in chip if c != me and all(topo.may_write(c, T.cores[q]) for q in (left, right))]
    near = [c for c in able if topo.die(c) == topo.die(me)]
    far = [c for c in able if topo.die(c) != topo.die(me)]
    return [(near[0], left, True, 0, D), (far[0], right, True, D, 0), (near[1], left, False, 0, D), (far[1], right, False, D, 0)]


def relay_program(g, core, T, topo):
    for r in range(len(T.cores)):
        me = T.cores[r]
        if (topo.host(me), topo.chip(me)) != (topo.host(core), topo.chip(core)):
            continue
        for relay, to, codes, _, col in plan(r, T, topo):
            if relay != core:
                continue
            dst = T.cores[to]
            rid, pid = topo.addr(dst, core)
            mask = topo.mask(core, dst)
            if codes:
                out, src = T.qr[:, col:col + D].bitcast(dt.uint8), T.rc[:, 0:D].bitcast(dt.uint8)
            else:
                out, src = T.sr[:, col:col + D], T.rp[:, 0:D]
            g.wait_ge(T.sem.rel, 4)
            g.remote_dma(out, src, T.sem.arr, T.sem.loc, pid, rid, mask)
            g.wait_ge(T.sem.loc, mask.bit_count())


def rank_program(g, core, T, topo):
    r = T.rank_of(core)
    if r is None:
        relay_program(g, core, T, topo)
        return
    S = T.sem
    v, s, pe, sy = g.vector, g.scalar, g.tensor, g.sync
    Relu, Copy = ActivationFunctionType.Relu, ActivationFunctionType.Copy
    pieces = plan(r, T, topo)
    n = len(T.cores)

    sy.dma_start(T.xh[:, 0:4 * D], T.x[:, 0:4 * D]).then_inc(S.lxh, 16)
    s.dma_start(T.xh[:, 4 * D:4 * H], T.x[:, 4 * (NC - D):4 * NC]).then_inc(S.lxh, 16)
    sy.dma_start(T.w1s[:, 0:1024], T.w1[:, 0:1024]).then_inc(S.lw0, 16)
    s.dma_start(T.xo[:], T.x[:]).then_inc(S.lx, 16)
    sy.dma_start(T.w1s[:, 1024:2048], T.w1[:, 1024:2048]).then_inc(S.lw1, 16)
    sy.wait_ge(S.iss, 1)
    sy.dma_start(T.wts[:], T.wt[:]).then_inc(S.lwt, 16)

    g.wait_ge(S.qxh, 1)
    for codes in (True, False):
        tr = []
        for k, (relay, _, c, col, _) in enumerate([p for p in pieces if p[2] == codes]):
            rid, pid = topo.addr(relay, core)
            if codes:
                src, dst = T.qxh[:, col:col + D].bitcast(dt.uint8), T.rc[:, 0:D].bitcast(dt.uint8)
            else:
                src, dst = T.sxh[:, col:col + D], T.rp[:, 0:D]
            tr.append(RemoteDMATransfer(dst_ids=[DstId(rid=rid, pnc=pid)], dma_engine_mask=engines(topo.mask(core, relay), 4 * k, 4),
                                        remote_sem=S.rel, src=src, dst=dst))
        g.remote_dma_fused(tr, local_sem=S.loc)
    g.sem_inc(S.iss, 1)
    g.wait_ge(S.loc, 16)

    v.wait_ge(S.lxh, 32)
    v.quantize_mx(T.qxh[:], T.sxh[:], T.xh[:]).then_inc(S.qxh, 1)
    v.wait_ge(S.lw0, 16)
    for i in (0, 1):
        v.quantize_mx(T.qw[:, 128 * i:128 * i + 128], T.sw[:, 128 * i:128 * i + 128], T.w1s[:, 512 * i:512 * i + 512]).then_inc(S["qw%d" % i], 1)
    v.wait_ge(S.lx, 16)
    v.quantize_mx(T.qx[:], T.sx[:], T.xo[:]).then_inc(S.qx, 1)
    v.wait_ge(S.lw1, 16)
    for i in (2, 3):
        v.quantize_mx(T.qw[:, 128 * i:128 * i + 128], T.sw[:, 128 * i:128 * i + 128], T.w1s[:, 512 * i:512 * i + 512]).then_inc(S["qw%d" % i], 1)

    pe.wait_ge(S.qx, 1)
    for i in range(4):
        pe.wait_ge(S["qw%d" % i], 1)
        pe.matmul_mx(T.zp[:, 512 * i:512 * i + NC], T.qw[:, 128 * i:128 * i + 128], T.sw[:, 128 * i:128 * i + 128],
                     T.qx[:], T.sx[:], True, True).then_inc(S["z%d" % i], 1)

    def act(b, z, n_, out, sem, done):
        if b % 2 == 0:
            s.wait_ge(sem, 1)
            s.activation(out[:, b:4 * n_:4], z[:, 512 * b:512 * b + n_], Relu, scale=C).then_inc(done, 1)
        else:
            v.wait_ge(sem, 1)
            v.tensor_scalar(out[:, b:4 * n_:4], z[:, 512 * b:512 * b + n_], 0.0, C, AluOpType.max, AluOpType.mult).then_inc(done, 1)
    for b in range(4):
        act(b, T.zp, NC, T.h, S["z%d" % b], S.act)
    v.wait_ge(S.act, 4)
    v.quantize_mx(T.qh[:], T.sh[:], T.h[:]).then_inc(S.qh, 1)
    v.wait_ge(S.lwt, 16)
    for i in range(3):
        v.quantize_mx(T.qt[:, 128 * i:128 * i + 128], T.st[:, 128 * i:128 * i + 128], T.wts[:, 512 * i:512 * i + 512]).then_inc(S.qwt, 1)

    def tap(bank, t, q, sc, a, w, start, stop):
        return pe.matmul_mx(T.zp[:, 512 * bank:512 * bank + w], T.qt[:, 128 * t:128 * t + 128], T.st[:, 128 * t:128 * t + 128],
                            q[:, a:a + w], sc[:, a:a + w], start, stop)
    pe.wait_ge(S.qh, 1)
    pe.wait_ge(S.qwt, 3)
    for t in range(3):
        m = tap(0, t, T.qh, T.sh, D * t, NC - H, t == 0, t == 2)
    m.then_inc(S.mA, 1)
    tap(1, 1, T.qh, T.sh, 0, H, True, False)
    tap(1, 2, T.qh, T.sh, D, H, False, False)
    tap(2, 0, T.qh, T.sh, NC - H - D, H, True, False)
    tap(2, 1, T.qh, T.sh, NC - H, H, False, False)
    s.wait_ge(S.mA, 1)
    s.activation(T.ya[:], T.zp[:, 0:NC - H], Copy).then_inc(S.cA, 1)
    sy.wait_ge(S.cA, 1)
    sy.dma_start(T.y[:, D:NC - D], T.ya[:]).then_inc(S.oAB, 16)

    arrive = 0
    for q in range(n):
        for relay, to, _, _, _ in plan(q, T, topo):
            if to == r:
                arrive += topo.mask(relay, core).bit_count()
    pe.wait_ge(S.arr, arrive)
    for i in range(4):
        pe.matmul_mx(T.zh[:, 512 * i:512 * i + H], T.qw[:, 128 * i:128 * i + 128], T.sw[:, 128 * i:128 * i + 128],
                     T.qr[:], T.sr[:], True, True).then_inc(S["zh%d" % i], 1)
    for b in range(4):
        act(b, T.zh, H, T.hh, S["zh%d" % b], S.acth)
    v.wait_ge(S.acth, 4)
    v.quantize_mx(T.qhh[:], T.shh[:], T.hh[:]).then_inc(S.qhh, 1)
    pe.wait_ge(S.qhh, 1)
    tap(1, 0, T.qhh, T.shh, 0, H, False, True).then_inc(S.mB, 1)
    tap(2, 2, T.qhh, T.shh, 0, H, False, True).then_inc(S.mC, 1)
    v.wait_ge(S.mB, 1)
    v.tensor_copy(T.yb[:], T.zp[:, 512:512 + D]).then_inc(S.cB, 1)
    s.wait_ge(S.mC, 1)
    s.activation(T.yc[:], T.zp[:, 1024 + D:1024 + H], Copy).then_inc(S.cC, 1)
    sy.wait_ge(S.cB, 1)
    sy.dma_start(T.y[:, 0:D], T.yb[:]).then_inc(S.oAB, 16)
    s.wait_ge(S.cC, 1)
    s.dma_start(T.y[:, NC - D:NC], T.yc[:]).then_inc(S.oC, 16)
    sy.wait_ge(S.oAB, 32)
    s.wait_ge(S.oC, 16)
